import numpy as np
import ml_dtypes


def mxq(x, axis, fmt="e4m3"):
    dtype, down = {"e4m3": (ml_dtypes.float8_e4m3fn, 7), "e5m2": (ml_dtypes.float8_e5m2, 14)}[fmt]
    v = np.moveaxis(np.asarray(x, np.float32).astype(ml_dtypes.bfloat16).astype(np.float64), axis, -1)
    blocks = v.reshape(v.shape[:-1] + (-1, 32))
    amax = np.abs(blocks).max(-1, keepdims=True)
    byte = np.maximum(np.where(amax > 0, np.frexp(amax)[1] - 1 + 127, 0) - down, 1)
    scale = np.exp2(byte - 127.0)
    codes = (blocks / scale).astype(np.float32).astype(dtype).astype(np.float64)
    return np.moveaxis((codes * scale).reshape(v.shape), -1, axis)


WIDE = False


def mx_kscale(k):
    if not WIDE:
        return np.ones(k)
    levels = np.array([10, -10, 5, -5, 0])
    if k % 512:
        return np.exp2(np.random.permutation(np.resize(levels, k // 32))).repeat(32)
    a = np.empty((k // 512, 16))
    for p in range(k // 512):
        a[p, :8] = np.random.permutation(np.resize(levels, 8))
        for g in range(8):
            far = levels[np.abs(levels - a[p, g]) >= 10]
            a[p, g + 8] = far[np.random.randint(len(far))]
    return np.exp2(a.ravel()).repeat(32)


def f64(x):
    return np.asarray(x).astype(np.float64)


def striped(idx):
    return np.tile(idx.reshape(-1, 16).T, (8, 1)).astype(np.uint16)


def unstriped(offs):
    return offs[:16].T.reshape(-1).astype(np.int64)


E2M1 = np.array([0.0, 0.5, 1.0, 1.5, 2.0, 3.0, 4.0, 6.0, -0.0, -0.5, -1.0, -1.5, -2.0, -3.0, -4.0, -6.0])


def pack_weight(w, fmt):
    k, n = w.shape
    w = f64(np.asarray(w, np.float32).astype(ml_dtypes.bfloat16)).reshape(k // 32, 32, n)
    amax = np.abs(w).max(1)
    if fmt == "e4m3":
        byte = np.frexp(amax)[1] - 1 + 127 - 7
    else:
        mant, ex = np.frexp(amax / 6.0)
        byte = np.where(mant > 0.5, ex, ex - 1) + 127
    byte = np.clip(np.where(amax > 0, byte, 1), 1, 254)
    scaled = (w * np.exp2(127.0 - byte)[:, None, :]).reshape(k, n).astype(np.float32)
    by_word = np.ascontiguousarray(scaled.reshape(k // 512, 128, 4, n).transpose(0, 1, 3, 2))
    if fmt == "e4m3":
        words = by_word.astype(ml_dtypes.float8_e4m3fn).view(np.uint8)
    else:
        c = by_word.astype(ml_dtypes.float4_e2m1fn).view(np.uint8) & 0xF
        words = (c[..., 0::2] | (c[..., 1::2] << 4)).reshape(k // 512, 128, 2 * n)
    return np.ascontiguousarray(words), np.ascontiguousarray(byte.astype(np.uint8).reshape(k // 512, 16, n))


def unpack_weight(words, scales, fmt):
    g, _, n = scales.shape
    words = np.ascontiguousarray(words).reshape(g, 128, n, -1)
    if fmt == "e4m3":
        vals = words.view(ml_dtypes.float8_e4m3fn).astype(np.float64)
    else:
        nib = np.empty((g, 128, n, 4), np.uint8)
        nib[..., 0::2] = words & 0xF
        nib[..., 1::2] = words >> 4
        vals = E2M1[nib]
    vals = vals * np.repeat(np.exp2(scales.astype(np.float64) - 127.0), 8, axis=1)[..., None]
    return vals.transpose(0, 1, 3, 2).reshape(g * 512, n)


def gelu(v):
    return 0.5 * v * (1.0 + np.tanh(np.sqrt(2.0 / np.pi) * (v + 0.044715 * v**3)))


def striped8(idx):
    return np.concatenate([v.reshape(-1, 16).T for v in idx]).astype(np.uint16)


def unstriped8(offs):
    return np.stack([offs[16 * g:16 * g + 16].T.reshape(-1) for g in range(8)]).astype(np.int64)


def heads(h, wgt, idx8):
    r = np.arange(h.shape[0])
    return wgt[r // 4 % 128] * h[r[:, None], idx8[r % 512 // 64]]


K, T, S, H, T2, P, N, G, E = 1024, 4096, 1024, 1024, 2048, 1024, 512, 128, 8

def setup_inputs():
    n = np.random.standard_normal
    s = mx_kscale(K)[:, None]
    u = mx_kscale(H)[:, None]
    tab_words, tab_scales = pack_weight(n((K, T)) * s, "e4m3")
    w2_words, w2_scales = pack_weight(1.2 * n((H, N)) / np.sqrt(H) / u, "e2m1")
    w3_words, w3_scales = pack_weight(0.7 * n((K, N)) / np.sqrt(K) / s, "e4m3")
    cells = np.stack([np.random.permutation(T2)[:P] for _ in range(E)])
    return {
        "tab_words": tab_words, "tab_scales": tab_scales,
        "offs": striped(np.random.permutation(T)[:S]),
        "w1": (1.2 * n((K, H)) / np.sqrt(K) / s).astype(np.float32),
        "b1": (0.5 * n(H)).astype(np.float32),
        "gain": (np.random.uniform(0.6, 1.4, H) * u[:, 0]).astype(np.float32),
        "page0": (0.8 * n((H, T2)) * u).astype(np.float32),
        "wgs": np.exp(0.3 * n((G, S))).astype(np.float32),
        "offs2": striped(np.random.permutation(T2)[:S]),
        "wgt": np.repeat(np.random.uniform(0.5, 2.0, (E, P)), G // E, axis=0).astype(np.float32),
        "offs3": striped8(cells),
        "w2_words": w2_words, "w2_scales": w2_scales,
        "w3_words": w3_words, "w3_scales": w3_scales,
    }

def reference(tab_words, tab_scales, offs, w1, b1, gain, page0, wgs, offs2, wgt, offs3,
              w2_words, w2_scales, w3_words, w3_scales):
    v = unpack_weight(tab_words, tab_scales, "e4m3")[:, unstriped(offs)]
    w2 = unpack_weight(w2_words, w2_scales, "e2m1")
    w3 = unpack_weight(w3_words, w3_scales, "e4m3")
    q = mxq(f64(w1), 0, "e4m3").T @ v
    h = f64(gain)[:, None] * np.tanh(q + f64(b1)[:, None])
    page = f64(page0).copy()
    page[:, unstriped(offs2)] = np.tile(f64(wgs), (H // G, 1)) * h
    x = heads(page, f64(wgt), unstriped8(offs3))
    y = w2.T @ mxq(x, 0, "e4m3")
    d = w3.T @ v
    return np.tanh(y) + d

@@ -1,0 +1,273 @@
+from contextlib import ExitStack
+
+import concourse.mybir as mybir
+from concourse.masks import make_identity
+
+K, T, S, H, T2, N = 1024, 4096, 1024, 1024, 2048, 512
+FLOPS = 2 * K * H * S + 2 * H * N * S + 2 * K * N * S
+
+F32 = mybir.dt.float32
+BF16 = mybir.dt.bfloat16
+I32 = mybir.dt.int32
+U32 = mybir.dt.uint32
+U16 = mybir.dt.uint16
+U8 = mybir.dt.uint8
+FP8X4 = mybir.dt.float8_e4m3fn_x4
+FP4X4 = mybir.dt.float4_e2m1fn_x4
+MULT = mybir.AluOpType.mult
+TANH = mybir.ActivationFunctionType.Tanh
+COPY = mybir.ActivationFunctionType.Copy
+
+P = 128
+PACK = 4
+K_PASS = P * PACK
+BANK = 512
+PER_COL = 16
+CHUNKS = (256, 256, 256, 128, 128)
+
+
+def tile_list_parking_echo_features_kernel(
+    tc, tab_words, tab_scales, offs, w1, b1, gain, page0, wgs, offs2, wgt, offs3,
+    w2_words, w2_scales, w3_words, w3_scales, out,
+):
+    nc = tc.nc
+    with ExitStack() as ctx:
+        lists = ctx.enter_context(tc.tile_pool(name="lists", bufs=1))
+        keep = ctx.enter_context(tc.tile_pool(name="keep", bufs=1))
+        ring = ctx.enter_context(tc.tile_pool(name="ring", bufs=2))
+        psum = ctx.enter_context(tc.psum_pool(name="psum", bufs=1))
+
+        list1 = lists.tile([P, S // PER_COL], U16, name="list1")
+        list2 = lists.tile([P, S // PER_COL], U16, name="list2")
+        list3 = lists.tile([P, S // PER_COL], U16, name="list3")
+
+        def entries(lst, j0, j1):
+            return lst[:, j0 // PER_COL : j1 // PER_COL]
+
+        def load_w1(a, b):
+            raw = keep.tile([P, PACK, K_PASS], F32, name=f"w1raw{a}{b}", tag=f"slab{2 * b + a}")
+            rows = w1[a * K_PASS : (a + 1) * K_PASS, b * K_PASS : (b + 1) * K_PASS]
+            nc.sync.dma_start(out=raw[:], in_=rows.rearrange("(p i) c -> p i c", i=PACK))
+            return raw
+
+        page_rows = page0.rearrange("(b p i) t -> b i p t", b=2, i=PACK)
+
+        def load_page(s):
+            tag = f"page{s}" if s < PACK else f"slab{s - PACK}"
+            page = keep.tile([P, T2], F32, name=f"page{s}", tag=tag)
+            nc.sync.dma_start(out=page[:], in_=page_rows[s // PACK, s % PACK])
+            return page
+
+        def load_tab(a):
+            words = keep.tile([P, T], I32, name=f"tab_w{a}", tag=f"tab_w{a}")
+            nc.sync.dma_start(out=words[:], in_=tab_words[a].rearrange("p t i -> p (t i)").bitcast(I32))
+            return words
+
+        wgs_rows = wgs.rearrange("(q i) j -> q i j", i=PACK)
+
+        tab_sc = keep.tile([P, T], U8, name="tab_sc", align_bytes=64)
+        nc.vector.memset(tab_sc[:].bitcast(I32), 0)
+        w_sc = keep.tile([P, 2, 2, N], U8, name="w_sc", align_bytes=64)
+        nc.gpsimd.memset(w_sc[:].rearrange("p w a n -> p (w a n)").bitcast(I32), 0)
+        ident = keep.tile([P, P], F32, name="ident")
+        make_identity(nc, ident[:])
+
+        nc.sync.dma_start(list1[:], offs)
+        w1raw = {(0, 0): load_w1(0, 0)}
+        for q in range(4):
+            nc.sync.dma_start(
+                out=tab_sc[32 * q : 32 * q + 8, :].bitcast(I32),
+                in_=tab_scales[:, 4 * q : 4 * q + 4, :].bitcast(I32),
+            )
+        w1raw[(1, 0)] = load_w1(1, 0)
+        tab_w = [load_tab(0)]
+        bias = keep.tile([P, 2, PACK], F32, name="bias")
+        nc.sync.dma_start(out=bias[:], in_=b1.rearrange("(b p i) -> p b i", b=2, i=PACK))
+        gains = keep.tile([P, 2, PACK], F32, name="gains")
+        nc.sync.dma_start(out=gains[:], in_=gain.rearrange("(b p i) -> p b i", b=2, i=PACK))
+        nc.sync.dma_start(list2[:], offs2)
+        tab_w.append(load_tab(1))
+        pages = [load_page(0)]
+        wgs_first = keep.tile([P, S], F32, name="wgs_first")
+        wgs_rest = keep.tile([P, PACK - 1, S], F32, name="wgs_rest")
+        for q in range(4):
+            nc.sync.dma_start(out=wgs_first[32 * q : 32 * q + 32, :], in_=wgs_rows[:, 0, :])
+        nc.sync.dma_start(list3[:], offs3)
+        wgt_sb = keep.tile([P, S], F32, name="wgt_sb")
+        nc.sync.dma_start(out=wgt_sb[:], in_=wgt)
+        pages.append(load_page(1))
+        for q in range(4):
+            nc.sync.dma_start(out=wgs_rest[32 * q : 32 * q + 32, :, :], in_=wgs_rows[:, 1:PACK, :])
+        for a in range(2):
+            w1raw[(a, 1)] = load_w1(a, 1)
+        pages.append(load_page(2))
+        pages.append(load_page(3))
+        w3_w = keep.tile([P, 2, N], I32, name="w3_w", align_bytes=64)
+        nc.sync.dma_start(out=w3_w[:], in_=w3_words.rearrange("a p c i -> p a (c i)").bitcast(I32))
+        w2_w = keep.tile([P, 2, 2 * N], U8, name="w2_w", align_bytes=64)
+        nc.sync.dma_start(out=w2_w[:].bitcast(I32), in_=w2_words.rearrange("a p c -> p a c").bitcast(I32))
+        for w, scales in enumerate((w3_scales, w2_scales)):
+            for q in range(4):
+                nc.sync.dma_start(
+                    out=w_sc[32 * q : 32 * q + 4, w, :, :].bitcast(I32),
+                    in_=scales[:, 4 * q : 4 * q + 4, :].rearrange("a r n -> r a n").bitcast(I32),
+                )
+
+        def wgs_plane(i):
+            return wgs_first[:] if i == 0 else wgs_rest[:, i - 1, :]
+
+        w1_codes, w1_sc = {}, {}
+
+        def round_w1(a, b, copy):
+            grouped = ring.tile([P, PACK * K_PASS], BF16, name="grouped", tag="grouped", align_bytes=64)
+            copy(
+                out=grouped[:].rearrange("p (t m i) -> p m i t", t=PACK, i=PACK),
+                in_=w1raw[(a, b)][:].rearrange("p i (m t) -> p m i t", t=PACK),
+            )
+            return grouped
+
+        def quantize_w1(a, b, grouped):
+            w1_codes[(a, b)] = keep.tile([P, K_PASS], U32, name=f"w1c{a}{b}", align_bytes=64)
+            w1_sc[(a, b)] = keep.tile([P, K_PASS], U8, name=f"w1s{a}{b}", align_bytes=64)
+            nc.vector.quantize_mx(out=w1_codes[(a, b)][:].bitcast(FP8X4), scales=w1_sc[(a, b)][:], in_=grouped[:])
+
+        staged = [round_w1(a, 0, nc.vector.tensor_copy) for a in range(2)]
+        for a in range(2):
+            quantize_w1(a, 0, staged[a])
+
+        v_sc = keep.tile([P, S], U8, name="v_sc", align_bytes=64)
+        nc.vector.tensor_copy(v_sc[:], tab_sc[:].indirect(list1[:]))
+        v_w = [keep.tile([P, S], U32, name=f"v_w{a}", align_bytes=64) for a in range(2)]
+        nc.vector.tensor_copy(v_w[0][:], tab_w[0][:].bitcast(U32).indirect(list1[:]))
+        for j0 in range(0, S, BANK):
+            nc.vector.tensor_copy(
+                v_w[1][:, j0 : j0 + BANK], tab_w[1][:].bitcast(U32).indirect(entries(list1, j0, j0 + BANK))
+            )
+
+        def make_h(s, h, gain_width):
+            b, i = divmod(s, PACK)
+            for j0 in range(0, S, BANK):
+                cols = slice(j0, j0 + BANK)
+                acc = psum.tile([P, BANK], F32, name="q_acc", tag="q_acc", bufs=3)
+                for a in range(2):
+                    nc.tensor.matmul_mx(
+                        out=acc[:],
+                        lhsT=w1_codes[(a, b)][:, i * P : (i + 1) * P].bitcast(FP8X4),
+                        lhsT_scale=w1_sc[(a, b)][:, i * P : (i + 1) * P],
+                        rhs=v_w[a][:, cols].bitcast(FP8X4),
+                        rhs_scale=v_sc[4 * a : P, cols],
+                        start=(a == 0),
+                        stop=(a == 1),
+                    )
+                nc.scalar.activation(out=h[:, cols], in_=acc[:], func=TANH, bias=bias[:, b, i : i + 1])
+                if (j0 + BANK) % gain_width == 0:
+                    done = slice(j0 + BANK - gain_width, j0 + BANK)
+                    nc.scalar.activation(out=h[:, done], in_=h[:, done], func=COPY, scale=gains[:, b, i : i + 1])
+
+        def scatter(s, h, j0, j1):
+            nc.vector.tensor_tensor(
+                pages[s][:].indirect(entries(list2, j0, j1)), h[:, j0:j1], wgs_plane(s % PACK)[:, j0:j1], MULT
+            )
+
+        def gather(s, dst, j0, j1):
+            nc.vector.tensor_tensor(dst, pages[s][:].indirect(entries(list3, j0, j1)), wgt_sb[:, j0:j1], MULT)
+
+        def interleave(planes, width):
+            grouped = ring.tile([P, PACK * K_PASS], BF16, name="grouped", tag="grouped", align_bytes=64)
+            nc.scalar.copy(
+                out=grouped[:, : PACK * width].rearrange("p (c e i) -> p c i e", e=4, i=PACK),
+                in_=planes.rearrange("p i (c e) -> p c i e", e=4),
+            )
+            return grouped
+
+        x_codes = [keep.tile([P, S], U32, name=f"x_codes{b}", align_bytes=64) for b in range(2)]
+        x_sc = [keep.tile([P, S], U8, name=f"x_sc{b}", align_bytes=64) for b in range(2)]
+
+        def quantize_x(b, grouped, j0, j1):
+            nc.vector.quantize_mx(
+                out=x_codes[b][:, j0:j1].bitcast(FP8X4), scales=x_sc[b][:, j0:j1], in_=grouped[:, : PACK * (j1 - j0)]
+            )
+
+        h_first = keep.tile([P, S], F32, name="h_first")
+        planes0 = keep.tile([P, PACK, S], F32, name="planes0")
+        h_last = [keep.tile([P, S], F32, name=f"h_last{n}") for n in range(3)]
+        h_of = [h_first[:]] + [planes0[:, i, :] for i in range(PACK)] + [h[:] for h in h_last]
+
+        make_h(0, h_of[0], BANK)
+        for j0 in range(0, S, BANK):
+            scatter(0, h_of[0], j0, j0 + BANK)
+        for s in range(1, PACK):
+            make_h(s, h_of[s], S)
+        staged = [round_w1(a, 1, nc.scalar.copy) for a in range(2)]
+        for a in range(2):
+            quantize_w1(a, 1, staged[a])
+        for s in range(PACK, 2 * PACK):
+            pages.append(load_page(s))
+            make_h(s, h_of[s], S)
+
+        d_t = keep.tile([P, S // P, N], F32, name="d_t", tag="tab_w0")
+        for jb in range(S // P):
+            cols = slice(jb * P, (jb + 1) * P)
+            acc = psum.tile([P, N], F32, name="t_acc", tag="t_acc", bufs=3)
+            for a in range(2):
+                nc.tensor.matmul_mx(
+                    out=acc[:],
+                    lhsT=v_w[a][:, cols].bitcast(FP8X4),
+                    lhsT_scale=v_sc[4 * a : P, cols],
+                    rhs=w3_w[:, a, :].bitcast(FP8X4),
+                    rhs_scale=w_sc[:, 0, a, :],
+                    start=(a == 0),
+                    stop=(a == 1),
+                )
+            nc.scalar.copy(out=d_t[:, jb, :], in_=acc[:])
+
+        for s in range(1, PACK + 1):
+            scatter(s, h_of[s], 0, S)
+            gather(s - 1, planes0[:, s - 1, :], 0, S)
+        for j0 in range(0, S, BANK):
+            quantize_x(0, interleave(planes0[:, :, j0 : j0 + BANK], BANK), j0, j0 + BANK)
+        for s in range(PACK + 1, 2 * PACK):
+            scatter(s, h_of[s], 0, S)
+
+        out_blocks = out.rearrange("(nb p) j -> p nb j", p=P)
+
+        def finish(jb):
+            cols = slice(jb * P, (jb + 1) * P)
+            acc = psum.tile([P, N], F32, name="t_acc", tag="t_acc", bufs=3)
+            for b in range(2):
+                nc.tensor.matmul_mx(
+                    out=acc[:],
+                    lhsT=x_codes[b][:, cols].bitcast(FP8X4),
+                    lhsT_scale=x_sc[b][:, cols],
+                    rhs=w2_w[:, b, :].bitcast(FP4X4),
+                    rhs_scale=w_sc[:, 1, b, :],
+                    start=(b == 0),
+                    stop=(b == 1),
+                )
+            bounded = ring.tile([P, N], F32, name="bounded")
+            nc.scalar.activation(out=bounded[:], in_=acc[:], func=TANH)
+            total = psum.tile([P, N // P, P], F32, name="total", tag="total", bufs=2)
+            terms = [(d_t[:, jb, :], nb) for nb in range(N // P)] + [(bounded[:], nb) for nb in range(N // P)]
+            for n, (term, nb) in enumerate(terms):
+                nc.tensor.matmul(
+                    out=total[:, nb, :],
+                    lhsT=term[:, nb * P : (nb + 1) * P],
+                    rhs=ident[:],
+                    start=(n == 0),
+                    stop=(n == len(terms) - 1),
+                    is_transpose=True,
+                )
+            result = ring.tile([P, N // P, P], F32, name="result", bufs=3)
+            nc.scalar.copy(out=result[:], in_=total[:])
+            nc.sync.dma_start(out=out_blocks[:, :, cols], in_=result[:])
+
+        spare = (h_of[-1], wgs_plane(PACK - 1))
+        j0 = 0
+        for c, width in enumerate(CHUNKS):
+            planes1 = spare[c % 2][:, : PACK * width].rearrange("p (i j) -> p i j", i=PACK)
+            for i in range(PACK):
+                gather(PACK + i, planes1[:, i, :], j0, j0 + width)
+            quantize_x(1, interleave(planes1, width), j0, j0 + width)
+            for jb in range(j0 // P, (j0 + width) // P):
+                finish(jb)
+            j0 = j0 + width

@@ -1,7 +1,6 @@
 from contextlib import ExitStack
 
 import concourse.mybir as mybir
-from concourse.masks import make_identity
 
 K, T, S, H, T2, N = 1024, 4096, 1024, 1024, 2048, 512
 FLOPS = 2 * K * H * S + 2 * H * N * S + 2 * K * N * S
@@ -15,6 +14,7 @@ U8 = mybir.dt.uint8
 FP8X4 = mybir.dt.float8_e4m3fn_x4
 FP4X4 = mybir.dt.float4_e2m1fn_x4
 MULT = mybir.AluOpType.mult
+ADD = mybir.AluOpType.add
 TANH = mybir.ActivationFunctionType.Tanh
 COPY = mybir.ActivationFunctionType.Copy
 
@@ -24,6 +24,7 @@ K_PASS = P * PACK
 BANK = 512
 PER_COL = 16
 CHUNKS = (256, 256, 256, 128, 128)
+LATE = 2
 
 
 def tile_list_parking_echo_features_kernel(
@@ -69,8 +70,6 @@ def tile_list_parking_echo_features_kernel(
         nc.vector.memset(tab_sc[:].bitcast(I32), 0)
         w_sc = keep.tile([P, 2, 2, N], U8, name="w_sc", align_bytes=64)
         nc.gpsimd.memset(w_sc[:].rearrange("p w a n -> p (w a n)").bitcast(I32), 0)
-        ident = keep.tile([P, P], F32, name="ident")
-        make_identity(nc, ident[:])
 
         nc.sync.dma_start(list1[:], offs)
         w1raw = {(0, 0): load_w1(0, 0)}
@@ -121,8 +120,8 @@ def tile_list_parking_echo_features_kernel(
         def round_w1(a, b, copy):
             grouped = ring.tile([P, PACK * K_PASS], BF16, name="grouped", tag="grouped", align_bytes=64)
             copy(
-                out=grouped[:].rearrange("p (t m i) -> p m i t", t=PACK, i=PACK),
-                in_=w1raw[(a, b)][:].rearrange("p i (m t) -> p m i t", t=PACK),
+                out=grouped[:].rearrange("p (t m i) -> p t m i", t=PACK, i=PACK),
+                in_=w1raw[(a, b)][:].rearrange("p i (m t) -> p t m i", t=PACK),
             )
             return grouped
 
@@ -131,7 +130,7 @@ def tile_list_parking_echo_features_kernel(
             w1_sc[(a, b)] = keep.tile([P, K_PASS], U8, name=f"w1s{a}{b}", align_bytes=64)
             nc.vector.quantize_mx(out=w1_codes[(a, b)][:].bitcast(FP8X4), scales=w1_sc[(a, b)][:], in_=grouped[:])
 
-        staged = [round_w1(a, 0, nc.vector.tensor_copy) for a in range(2)]
+        staged = [round_w1(0, 0, nc.vector.tensor_copy), round_w1(1, 0, nc.scalar.copy)]
         for a in range(2):
             quantize_w1(a, 0, staged[a])
 
@@ -144,11 +143,18 @@ def tile_list_parking_echo_features_kernel(
                 v_w[1][:, j0 : j0 + BANK], tab_w[1][:].bitcast(U32).indirect(entries(list1, j0, j0 + BANK))
             )
 
+        banks_used = []
+
+        def next_bank():
+            bank = psum.tile([P, BANK], F32, name="bank", tag=f"bank{len(banks_used) % 8}")
+            banks_used.append(bank)
+            return bank
+
         def make_h(s, h, gain_width):
             b, i = divmod(s, PACK)
             for j0 in range(0, S, BANK):
                 cols = slice(j0, j0 + BANK)
-                acc = psum.tile([P, BANK], F32, name="q_acc", tag="q_acc", bufs=3)
+                acc = next_bank()
                 for a in range(2):
                     nc.tensor.matmul_mx(
                         out=acc[:],
@@ -189,9 +195,12 @@ def tile_list_parking_echo_features_kernel(
             )
 
         h_first = keep.tile([P, S], F32, name="h_first")
-        planes0 = keep.tile([P, PACK, S], F32, name="planes0")
-        h_last = [keep.tile([P, S], F32, name=f"h_last{n}") for n in range(3)]
-        h_of = [h_first[:]] + [planes0[:, i, :] for i in range(PACK)] + [h[:] for h in h_last]
+        planes = [keep.tile([P, PACK, S], F32, name=f"planes{b}") for b in range(2)]
+
+        def plane(s):
+            return planes[s // PACK][:, s % PACK, :]
+
+        h_of = [h_first[:]] + [plane(s) for s in range(2 * PACK - 1)]
 
         make_h(0, h_of[0], BANK)
         for j0 in range(0, S, BANK):
@@ -205,69 +214,64 @@ def tile_list_parking_echo_features_kernel(
             pages.append(load_page(s))
             make_h(s, h_of[s], S)
 
-        d_t = keep.tile([P, S // P, N], F32, name="d_t", tag="tab_w0")
-        for jb in range(S // P):
-            cols = slice(jb * P, (jb + 1) * P)
-            acc = psum.tile([P, N], F32, name="t_acc", tag="t_acc", bufs=3)
-            for a in range(2):
+        total = keep.tile([P, N // P, S], F32, name="total", tag="tab_w0")
+        for nb in range(N // P):
+            for j0 in range(0, S, BANK):
+                cols = slice(j0, j0 + BANK)
+                acc = next_bank()
+                for a in range(2):
+                    nc.tensor.matmul_mx(
+                        out=acc[:],
+                        lhsT=w3_w[:, a, nb * P : (nb + 1) * P].bitcast(FP8X4),
+                        lhsT_scale=w_sc[:, 0, a, nb * P : (nb + 1) * P],
+                        rhs=v_w[a][:, cols].bitcast(FP8X4),
+                        rhs_scale=v_sc[4 * a : P, cols],
+                        start=(a == 0),
+                        stop=(a == 1),
+                    )
+                nc.scalar.copy(out=total[:, nb, cols], in_=acc[:])
+
+        def y_pass(b, bank, nbs, j0, j1):
+            for n, nb in enumerate(nbs):
                 nc.tensor.matmul_mx(
-                    out=acc[:],
-                    lhsT=v_w[a][:, cols].bitcast(FP8X4),
-                    lhsT_scale=v_sc[4 * a : P, cols],
-                    rhs=w3_w[:, a, :].bitcast(FP8X4),
-                    rhs_scale=w_sc[:, 0, a, :],
-                    start=(a == 0),
-                    stop=(a == 1),
+                    out=bank[:, n * (j1 - j0) : (n + 1) * (j1 - j0)],
+                    lhsT=w2_w[:, b, 2 * nb * P : 2 * (nb + 1) * P].bitcast(FP4X4),
+                    lhsT_scale=w_sc[:, 1, b, nb * P : (nb + 1) * P],
+                    rhs=x_codes[b][:, j0:j1].bitcast(FP8X4),
+                    rhs_scale=x_sc[b][:, j0:j1],
+                    start=(b == 0 and n == 0),
+                    stop=(b == 1 and n == len(nbs) - 1),
                 )
-            nc.scalar.copy(out=d_t[:, jb, :], in_=acc[:])
 
         for s in range(1, PACK + 1):
             scatter(s, h_of[s], 0, S)
-            gather(s - 1, planes0[:, s - 1, :], 0, S)
+            gather(s - 1, plane(s - 1), 0, S)
         for j0 in range(0, S, BANK):
-            quantize_x(0, interleave(planes0[:, :, j0 : j0 + BANK], BANK), j0, j0 + BANK)
+            quantize_x(0, interleave(planes[0][:, :, j0 : j0 + BANK], BANK), j0, j0 + BANK)
+
+        starts = [sum(CHUNKS[:c]) for c in range(len(CHUNKS))]
+        y_banks = []
+        for j0, width in zip(starts, CHUNKS):
+            per_bank = BANK // width
+            y_banks.append([(next_bank(), range(nb, nb + per_bank)) for nb in range(0, N // P, per_bank)])
+            for bank, nbs in y_banks[-1]:
+                y_pass(0, bank, nbs, j0, j0 + width)
+
         for s in range(PACK + 1, 2 * PACK):
             scatter(s, h_of[s], 0, S)
+            if s - 1 < 2 * PACK - LATE:
+                gather(s - 1, plane(s - 1), 0, S)
 
         out_blocks = out.rearrange("(nb p) j -> p nb j", p=P)
-
-        def finish(jb):
-            cols = slice(jb * P, (jb + 1) * P)
-            acc = psum.tile([P, N], F32, name="t_acc", tag="t_acc", bufs=3)
-            for b in range(2):
-                nc.tensor.matmul_mx(
-                    out=acc[:],
-                    lhsT=x_codes[b][:, cols].bitcast(FP8X4),
-                    lhsT_scale=x_sc[b][:, cols],
-                    rhs=w2_w[:, b, :].bitcast(FP4X4),
-                    rhs_scale=w_sc[:, 1, b, :],
-                    start=(b == 0),
-                    stop=(b == 1),
-                )
-            bounded = ring.tile([P, N], F32, name="bounded")
-            nc.scalar.activation(out=bounded[:], in_=acc[:], func=TANH)
-            total = psum.tile([P, N // P, P], F32, name="total", tag="total", bufs=2)
-            terms = [(d_t[:, jb, :], nb) for nb in range(N // P)] + [(bounded[:], nb) for nb in range(N // P)]
-            for n, (term, nb) in enumerate(terms):
-                nc.tensor.matmul(
-                    out=total[:, nb, :],
-                    lhsT=term[:, nb * P : (nb + 1) * P],
-                    rhs=ident[:],
-                    start=(n == 0),
-                    stop=(n == len(terms) - 1),
-                    is_transpose=True,
-                )
-            result = ring.tile([P, N // P, P], F32, name="result", bufs=3)
-            nc.scalar.copy(out=result[:], in_=total[:])
-            nc.sync.dma_start(out=out_blocks[:, :, cols], in_=result[:])
-
-        spare = (h_of[-1], wgs_plane(PACK - 1))
-        j0 = 0
-        for c, width in enumerate(CHUNKS):
-            planes1 = spare[c % 2][:, : PACK * width].rearrange("p (i j) -> p i j", i=PACK)
-            for i in range(PACK):
-                gather(PACK + i, planes1[:, i, :], j0, j0 + width)
-            quantize_x(1, interleave(planes1, width), j0, j0 + width)
-            for jb in range(j0 // P, (j0 + width) // P):
-                finish(jb)
-            j0 = j0 + width
+        for j0, width, chunk_banks in zip(starts, CHUNKS, y_banks):
+            j1 = j0 + width
+            for s in range(2 * PACK - LATE, 2 * PACK):
+                gather(s, plane(s)[:, j0:j1], j0, j1)
+            quantize_x(1, interleave(planes[1][:, :, j0:j1], width), j0, j1)
+            for bank, nbs in chunk_banks:
+                y_pass(1, bank, nbs, j0, j1)
+                bounded = ring.tile([P, BANK], F32, name="bounded", bufs=3)
+                nc.scalar.activation(out=bounded[:], in_=bank[:], func=TANH)
+                part = total[:, nbs.start : nbs.stop, j0:j1]
+                nc.vector.tensor_tensor(part, bounded[:].rearrange("p (n j) -> p n j", j=width), part, ADD)
+                nc.sync.dma_start(out=out_blocks[:, nbs.start : nbs.stop, j0:j1], in_=part)

@@ -24,7 +24,7 @@ K_PASS = P * PACK
 BANK = 512
 PER_COL = 16
 CHUNKS = (256, 256, 256, 128, 128)
-LATE = 2
+LATE = 3
 
 
 def tile_list_parking_echo_features_kernel(
@@ -89,17 +89,17 @@ def tile_list_parking_echo_features_kernel(
         pages = [load_page(0)]
         wgs_first = keep.tile([P, S], F32, name="wgs_first")
         wgs_rest = keep.tile([P, PACK - 1, S], F32, name="wgs_rest")
-        for q in range(4):
+        for q in (0, 2, 1, 3):
             nc.sync.dma_start(out=wgs_first[32 * q : 32 * q + 32, :], in_=wgs_rows[:, 0, :])
         nc.sync.dma_start(list3[:], offs3)
         wgt_sb = keep.tile([P, S], F32, name="wgt_sb")
         nc.sync.dma_start(out=wgt_sb[:], in_=wgt)
         pages.append(load_page(1))
-        for q in range(4):
+        for q in (0, 2, 1, 3):
             nc.sync.dma_start(out=wgs_rest[32 * q : 32 * q + 32, :, :], in_=wgs_rows[:, 1:PACK, :])
+        pages.append(load_page(2))
         for a in range(2):
             w1raw[(a, 1)] = load_w1(a, 1)
-        pages.append(load_page(2))
         pages.append(load_page(3))
         w3_w = keep.tile([P, 2, N], I32, name="w3_w", align_bytes=64)
         nc.sync.dma_start(out=w3_w[:], in_=w3_words.rearrange("a p c i -> p a (c i)").bitcast(I32))
@@ -181,8 +181,8 @@ def tile_list_parking_echo_features_kernel(
         def interleave(planes, width):
             grouped = ring.tile([P, PACK * K_PASS], BF16, name="grouped", tag="grouped", align_bytes=64)
             nc.scalar.copy(
-                out=grouped[:, : PACK * width].rearrange("p (c e i) -> p c i e", e=4, i=PACK),
-                in_=planes.rearrange("p i (c e) -> p c i e", e=4),
+                out=grouped[:, : PACK * width].rearrange("p (j i) -> p j i", i=PACK),
+                in_=planes.rearrange("p i j -> p j i"),
             )
             return grouped
 

@@ -24,7 +24,7 @@ K_PASS = P * PACK
 BANK = 512
 PER_COL = 16
 CHUNKS = (256, 256, 256, 128, 128)
-LATE = 3
+FIRST_PARTS = ((0, 512), (512, 1024))
 
 
 def tile_list_parking_echo_features_kernel(
@@ -66,6 +66,12 @@ def tile_list_parking_echo_features_kernel(
 
         wgs_rows = wgs.rearrange("(q i) j -> q i j", i=PACK)
 
+        def load_wgs(i):
+            dealt = keep.tile([P, S], F32, name=f"wgs{i}")
+            for q in (0, 2, 1, 3):
+                nc.sync.dma_start(out=dealt[32 * q : 32 * q + 32, :], in_=wgs_rows[:, i, :])
+            return dealt
+
         tab_sc = keep.tile([P, T], U8, name="tab_sc", align_bytes=64)
         nc.vector.memset(tab_sc[:].bitcast(I32), 0)
         w_sc = keep.tile([P, 2, 2, N], U8, name="w_sc", align_bytes=64)
@@ -87,20 +93,17 @@ def tile_list_parking_echo_features_kernel(
         nc.sync.dma_start(list2[:], offs2)
         tab_w.append(load_tab(1))
         pages = [load_page(0)]
-        wgs_first = keep.tile([P, S], F32, name="wgs_first")
-        wgs_rest = keep.tile([P, PACK - 1, S], F32, name="wgs_rest")
-        for q in (0, 2, 1, 3):
-            nc.sync.dma_start(out=wgs_first[32 * q : 32 * q + 32, :], in_=wgs_rows[:, 0, :])
+        wgs_sb = [load_wgs(0)]
+        pages.append(load_page(1))
+        wgs_sb.append(load_wgs(1))
+        for s in (2, 3):
+            pages.append(load_page(s))
+            wgs_sb.append(load_wgs(s))
+        for a in range(2):
+            w1raw[(a, 1)] = load_w1(a, 1)
         nc.sync.dma_start(list3[:], offs3)
         wgt_sb = keep.tile([P, S], F32, name="wgt_sb")
         nc.sync.dma_start(out=wgt_sb[:], in_=wgt)
-        pages.append(load_page(1))
-        for q in (0, 2, 1, 3):
-            nc.sync.dma_start(out=wgs_rest[32 * q : 32 * q + 32, :, :], in_=wgs_rows[:, 1:PACK, :])
-        pages.append(load_page(2))
-        for a in range(2):
-            w1raw[(a, 1)] = load_w1(a, 1)
-        pages.append(load_page(3))
         w3_w = keep.tile([P, 2, N], I32, name="w3_w", align_bytes=64)
         nc.sync.dma_start(out=w3_w[:], in_=w3_words.rearrange("a p c i -> p a (c i)").bitcast(I32))
         w2_w = keep.tile([P, 2, 2 * N], U8, name="w2_w", align_bytes=64)
@@ -112,27 +115,22 @@ def tile_list_parking_echo_features_kernel(
                     in_=scales[:, 4 * q : 4 * q + 4, :].rearrange("a r n -> r a n").bitcast(I32),
                 )
 
-        def wgs_plane(i):
-            return wgs_first[:] if i == 0 else wgs_rest[:, i - 1, :]
+        w1_codes = [keep.tile([P, 2, K_PASS], U32, name=f"w1_codes{b}", align_bytes=64) for b in range(2)]
+        w1_sc = [keep.tile([P, 2, K_PASS], U8, name=f"w1_sc{b}", align_bytes=64) for b in range(2)]
 
-        w1_codes, w1_sc = {}, {}
-
-        def round_w1(a, b, copy):
-            grouped = ring.tile([P, PACK * K_PASS], BF16, name="grouped", tag="grouped", align_bytes=64)
+        def round_w1(a, b, grouped, copy):
             copy(
-                out=grouped[:].rearrange("p (t m i) -> p t m i", t=PACK, i=PACK),
+                out=grouped.rearrange("p (t m i) -> p t m i", t=PACK, i=PACK),
                 in_=w1raw[(a, b)][:].rearrange("p i (m t) -> p t m i", t=PACK),
             )
-            return grouped
 
-        def quantize_w1(a, b, grouped):
-            w1_codes[(a, b)] = keep.tile([P, K_PASS], U32, name=f"w1c{a}{b}", align_bytes=64)
-            w1_sc[(a, b)] = keep.tile([P, K_PASS], U8, name=f"w1s{a}{b}", align_bytes=64)
-            nc.vector.quantize_mx(out=w1_codes[(a, b)][:].bitcast(FP8X4), scales=w1_sc[(a, b)][:], in_=grouped[:])
-
-        staged = [round_w1(0, 0, nc.vector.tensor_copy), round_w1(1, 0, nc.scalar.copy)]
+        staged = [
+            ring.tile([P, PACK * K_PASS], BF16, name="grouped", tag="grouped", align_bytes=64) for a in range(2)
+        ]
+        round_w1(0, 0, staged[0][:], nc.vector.tensor_copy)
+        round_w1(1, 0, staged[1][:], nc.scalar.copy)
         for a in range(2):
-            quantize_w1(a, 0, staged[a])
+            nc.vector.quantize_mx(out=w1_codes[0][:, a, :].bitcast(FP8X4), scales=w1_sc[0][:, a, :], in_=staged[a][:])
 
         v_sc = keep.tile([P, S], U8, name="v_sc", align_bytes=64)
         nc.vector.tensor_copy(v_sc[:], tab_sc[:].indirect(list1[:]))
@@ -150,29 +148,33 @@ def tile_list_parking_echo_features_kernel(
             banks_used.append(bank)
             return bank
 
-        def make_h(s, h, gain_width):
+        def tanh_part(s, h, j0, j1):
             b, i = divmod(s, PACK)
+            acc = next_bank()
+            for a in range(2):
+                nc.tensor.matmul_mx(
+                    out=acc[:, : j1 - j0],
+                    lhsT=w1_codes[b][:, a, i * P : (i + 1) * P].bitcast(FP8X4),
+                    lhsT_scale=w1_sc[b][:, a, i * P : (i + 1) * P],
+                    rhs=v_w[a][:, j0:j1].bitcast(FP8X4),
+                    rhs_scale=v_sc[4 * a : P, j0:j1],
+                    start=(a == 0),
+                    stop=(a == 1),
+                )
+            nc.scalar.activation(out=h[:, j0:j1], in_=acc[:, : j1 - j0], func=TANH, bias=bias[:, b, i : i + 1])
+
+        def weigh(s, h, j0, j1):
+            b, i = divmod(s, PACK)
+            nc.scalar.activation(out=h[:, j0:j1], in_=h[:, j0:j1], func=COPY, scale=gains[:, b, i : i + 1])
+
+        def make_h(s, h):
             for j0 in range(0, S, BANK):
-                cols = slice(j0, j0 + BANK)
-                acc = next_bank()
-                for a in range(2):
-                    nc.tensor.matmul_mx(
-                        out=acc[:],
-                        lhsT=w1_codes[(a, b)][:, i * P : (i + 1) * P].bitcast(FP8X4),
-                        lhsT_scale=w1_sc[(a, b)][:, i * P : (i + 1) * P],
-                        rhs=v_w[a][:, cols].bitcast(FP8X4),
-                        rhs_scale=v_sc[4 * a : P, cols],
-                        start=(a == 0),
-                        stop=(a == 1),
-                    )
-                nc.scalar.activation(out=h[:, cols], in_=acc[:], func=TANH, bias=bias[:, b, i : i + 1])
-                if (j0 + BANK) % gain_width == 0:
-                    done = slice(j0 + BANK - gain_width, j0 + BANK)
-                    nc.scalar.activation(out=h[:, done], in_=h[:, done], func=COPY, scale=gains[:, b, i : i + 1])
+                tanh_part(s, h, j0, j0 + BANK)
+            weigh(s, h, 0, S)
 
         def scatter(s, h, j0, j1):
             nc.vector.tensor_tensor(
-                pages[s][:].indirect(entries(list2, j0, j1)), h[:, j0:j1], wgs_plane(s % PACK)[:, j0:j1], MULT
+                pages[s][:].indirect(entries(list2, j0, j1)), h[:, j0:j1], wgs_sb[s % PACK][:, j0:j1], MULT
             )
 
         def gather(s, dst, j0, j1):
@@ -194,25 +196,31 @@ def tile_list_parking_echo_features_kernel(
                 out=x_codes[b][:, j0:j1].bitcast(FP8X4), scales=x_sc[b][:, j0:j1], in_=grouped[:, : PACK * (j1 - j0)]
             )
 
-        h_first = keep.tile([P, S], F32, name="h_first")
-        planes = [keep.tile([P, PACK, S], F32, name=f"planes{b}") for b in range(2)]
+        planes = keep.tile([P, PACK, S], F32, name="planes", align_bytes=64)
 
-        def plane(s):
-            return planes[s // PACK][:, s % PACK, :]
+        def h_buffer(s):
+            if s in (3, 4):
+                return planes[:, s - 1, :]
+            return keep.tile([P, S], F32, name=f"h{s}", tag=f"h{s % 5}")[:]
 
-        h_of = [h_first[:]] + [plane(s) for s in range(2 * PACK - 1)]
+        h_of = [h_buffer(s) for s in range(2 * PACK)]
 
-        make_h(0, h_of[0], BANK)
-        for j0 in range(0, S, BANK):
-            scatter(0, h_of[0], j0, j0 + BANK)
+        for j0, j1 in FIRST_PARTS:
+            tanh_part(0, h_of[0], j0, j1)
+            weigh(0, h_of[0], j0, j1)
+            scatter(0, h_of[0], j0, j1)
         for s in range(1, PACK):
-            make_h(s, h_of[s], S)
-        staged = [round_w1(a, 1, nc.scalar.copy) for a in range(2)]
+            make_h(s, h_of[s])
         for a in range(2):
-            quantize_w1(a, 1, staged[a])
+            round_w1(a, 1, planes[:, a, :].bitcast(BF16), nc.scalar.copy)
+        nc.vector.quantize_mx(
+            out=w1_codes[1][:].rearrange("p a c -> p (a c)").bitcast(FP8X4),
+            scales=w1_sc[1][:].rearrange("p a c -> p (a c)"),
+            in_=planes[:, 0:2, :].rearrange("p a j -> p (a j)").bitcast(BF16),
+        )
         for s in range(PACK, 2 * PACK):
             pages.append(load_page(s))
-            make_h(s, h_of[s], S)
+            make_h(s, h_of[s])
 
         total = keep.tile([P, N // P, S], F32, name="total", tag="tab_w0")
         for nb in range(N // P):
@@ -245,9 +253,9 @@ def tile_list_parking_echo_features_kernel(
 
         for s in range(1, PACK + 1):
             scatter(s, h_of[s], 0, S)
-            gather(s - 1, plane(s - 1), 0, S)
+            gather(s - 1, planes[:, s - 1, :], 0, S)
         for j0 in range(0, S, BANK):
-            quantize_x(0, interleave(planes[0][:, :, j0 : j0 + BANK], BANK), j0, j0 + BANK)
+            quantize_x(0, interleave(planes[:, :, j0 : j0 + BANK], BANK), j0, j0 + BANK)
 
         starts = [sum(CHUNKS[:c]) for c in range(len(CHUNKS))]
         y_banks = []
@@ -259,15 +267,15 @@ def tile_list_parking_echo_features_kernel(
 
         for s in range(PACK + 1, 2 * PACK):
             scatter(s, h_of[s], 0, S)
-            if s - 1 < 2 * PACK - LATE:
-                gather(s - 1, plane(s - 1), 0, S)
 
         out_blocks = out.rearrange("(nb p) j -> p nb j", p=P)
-        for j0, width, chunk_banks in zip(starts, CHUNKS, y_banks):
+        spare = (h_of[-1], wgs_sb[-1][:])
+        for c, (j0, width, chunk_banks) in enumerate(zip(starts, CHUNKS, y_banks)):
             j1 = j0 + width
-            for s in range(2 * PACK - LATE, 2 * PACK):
-                gather(s, plane(s)[:, j0:j1], j0, j1)
-            quantize_x(1, interleave(planes[1][:, :, j0:j1], width), j0, j1)
+            late = spare[c % 2][:, : PACK * width].rearrange("p (i j) -> p i j", i=PACK)
+            for i in range(PACK):
+                gather(PACK + i, late[:, i, :], j0, j1)
+            quantize_x(1, interleave(late, width), j0, j1)
             for bank, nbs in chunk_banks:
                 y_pass(1, bank, nbs, j0, j1)
                 bounded = ring.tile([P, BANK], F32, name="bounded", bufs=3)

from contextlib import ExitStack

import concourse.mybir as mybir

K, T, S, H, T2, N = 1024, 4096, 1024, 1024, 2048, 512
FLOPS = 2 * K * H * S + 2 * H * N * S + 2 * K * N * S

F32 = mybir.dt.float32
BF16 = mybir.dt.bfloat16
I32 = mybir.dt.int32
U32 = mybir.dt.uint32
U16 = mybir.dt.uint16
U8 = mybir.dt.uint8
FP8X4 = mybir.dt.float8_e4m3fn_x4
FP4X4 = mybir.dt.float4_e2m1fn_x4
MULT = mybir.AluOpType.mult
ADD = mybir.AluOpType.add
TANH = mybir.ActivationFunctionType.Tanh
COPY = mybir.ActivationFunctionType.Copy

P = 128
PACK = 4
K_PASS = P * PACK
BANK = 512
PER_COL = 16
CHUNKS = (256, 256, 256, 128, 128)
FIRST_PARTS = ((0, 512), (512, 1024))


def tile_list_parking_echo_features_kernel(
    tc, tab_words, tab_scales, offs, w1, b1, gain, page0, wgs, offs2, wgt, offs3,
    w2_words, w2_scales, w3_words, w3_scales, out,
):
    nc = tc.nc
    with ExitStack() as ctx:
        lists = ctx.enter_context(tc.tile_pool(name="lists", bufs=1))
        keep = ctx.enter_context(tc.tile_pool(name="keep", bufs=1))
        ring = ctx.enter_context(tc.tile_pool(name="ring", bufs=2))
        psum = ctx.enter_context(tc.psum_pool(name="psum", bufs=1))

        list1 = lists.tile([P, S // PER_COL], U16, name="list1")
        list2 = lists.tile([P, S // PER_COL], U16, name="list2")
        list3 = lists.tile([P, S // PER_COL], U16, name="list3")

        def entries(lst, j0, j1):
            return lst[:, j0 // PER_COL : j1 // PER_COL]

        def load_w1(a, b):
            raw = keep.tile([P, PACK, K_PASS], F32, name=f"w1raw{a}{b}", tag=f"slab{2 * b + a}")
            rows = w1[a * K_PASS : (a + 1) * K_PASS, b * K_PASS : (b + 1) * K_PASS]
            nc.sync.dma_start(out=raw[:], in_=rows.rearrange("(p i) c -> p i c", i=PACK))
            return raw

        page_rows = page0.rearrange("(b p i) t -> b i p t", b=2, i=PACK)

        def load_page(s):
            tag = f"page{s}" if s < PACK else f"slab{s - PACK}"
            page = keep.tile([P, T2], F32, name=f"page{s}", tag=tag)
            nc.sync.dma_start(out=page[:], in_=page_rows[s // PACK, s % PACK])
            return page

        def load_tab(a):
            words = keep.tile([P, T], I32, name=f"tab_w{a}", tag=f"tab_w{a}")
            nc.sync.dma_start(out=words[:], in_=tab_words[a].rearrange("p t i -> p (t i)").bitcast(I32))
            return words

        wgs_rows = wgs.rearrange("(q i) j -> q i j", i=PACK)

        def load_wgs(i):
            dealt = keep.tile([P, S], F32, name=f"wgs{i}")
            for q in (0, 2, 1, 3):
                nc.sync.dma_start(out=dealt[32 * q : 32 * q + 32, :], in_=wgs_rows[:, i, :])
            return dealt

        tab_sc = keep.tile([P, T], U8, name="tab_sc", align_bytes=64)
        nc.vector.memset(tab_sc[:].bitcast(I32), 0)
        w_sc = keep.tile([P, 2, 2, N], U8, name="w_sc", align_bytes=64)
        nc.gpsimd.memset(w_sc[:].rearrange("p w a n -> p (w a n)").bitcast(I32), 0)

        nc.sync.dma_start(list1[:], offs)
        w1raw = {(0, 0): load_w1(0, 0)}
        for q in range(4):
            nc.sync.dma_start(
                out=tab_sc[32 * q : 32 * q + 8, :].bitcast(I32),
                in_=tab_scales[:, 4 * q : 4 * q + 4, :].bitcast(I32),
            )
        w1raw[(1, 0)] = load_w1(1, 0)
        tab_w = [load_tab(0)]
        bias = keep.tile([P, 2, PACK], F32, name="bias")
        nc.sync.dma_start(out=bias[:], in_=b1.rearrange("(b p i) -> p b i", b=2, i=PACK))
        gains = keep.tile([P, 2, PACK], F32, name="gains")
        nc.sync.dma_start(out=gains[:], in_=gain.rearrange("(b p i) -> p b i", b=2, i=PACK))
        nc.sync.dma_start(list2[:], offs2)
        tab_w.append(load_tab(1))
        pages = [load_page(0)]
        wgs_sb = [load_wgs(0)]
        pages.append(load_page(1))
        wgs_sb.append(load_wgs(1))
        for s in (2, 3):
            pages.append(load_page(s))
            wgs_sb.append(load_wgs(s))
        for a in range(2):
            w1raw[(a, 1)] = load_w1(a, 1)
        nc.sync.dma_start(list3[:], offs3)
        wgt_sb = keep.tile([P, S], F32, name="wgt_sb")
        nc.sync.dma_start(out=wgt_sb[:], in_=wgt)
        w3_w = keep.tile([P, 2, N], I32, name="w3_w", align_bytes=64)
        nc.sync.dma_start(out=w3_w[:], in_=w3_words.rearrange("a p c i -> p a (c i)").bitcast(I32))
        w2_w = keep.tile([P, 2, 2 * N], U8, name="w2_w", align_bytes=64)
        nc.sync.dma_start(out=w2_w[:].bitcast(I32), in_=w2_words.rearrange("a p c -> p a c").bitcast(I32))
        for w, scales in enumerate((w3_scales, w2_scales)):
            for q in range(4):
                nc.sync.dma_start(
                    out=w_sc[32 * q : 32 * q + 4, w, :, :].bitcast(I32),
                    in_=scales[:, 4 * q : 4 * q + 4, :].rearrange("a r n -> r a n").bitcast(I32),
                )

        w1_codes = [keep.tile([P, 2, K_PASS], U32, name=f"w1_codes{b}", align_bytes=64) for b in range(2)]
        w1_sc = [keep.tile([P, 2, K_PASS], U8, name=f"w1_sc{b}", align_bytes=64) for b in range(2)]

        def round_w1(a, b, grouped, copy):
            copy(
                out=grouped.rearrange("p (t m i) -> p t m i", t=PACK, i=PACK),
                in_=w1raw[(a, b)][:].rearrange("p i (m t) -> p t m i", t=PACK),
            )

        staged = [
            ring.tile([P, PACK * K_PASS], BF16, name="grouped", tag="grouped", align_bytes=64) for a in range(2)
        ]
        round_w1(0, 0, staged[0][:], nc.vector.tensor_copy)
        round_w1(1, 0, staged[1][:], nc.scalar.copy)
        for a in range(2):
            nc.vector.quantize_mx(out=w1_codes[0][:, a, :].bitcast(FP8X4), scales=w1_sc[0][:, a, :], in_=staged[a][:])

        v_sc = keep.tile([P, S], U8, name="v_sc", align_bytes=64)
        nc.vector.tensor_copy(v_sc[:], tab_sc[:].indirect(list1[:]))
        v_w = [keep.tile([P, S], U32, name=f"v_w{a}", align_bytes=64) for a in range(2)]
        nc.vector.tensor_copy(v_w[0][:], tab_w[0][:].bitcast(U32).indirect(list1[:]))
        for j0 in range(0, S, BANK):
            nc.vector.tensor_copy(
                v_w[1][:, j0 : j0 + BANK], tab_w[1][:].bitcast(U32).indirect(entries(list1, j0, j0 + BANK))
            )

        banks_used = []

        def next_bank():
            bank = psum.tile([P, BANK], F32, name="bank", tag=f"bank{len(banks_used) % 8}")
            banks_used.append(bank)
            return bank

        def tanh_part(s, h, j0, j1):
            b, i = divmod(s, PACK)
            acc = next_bank()
            for a in range(2):
                nc.tensor.matmul_mx(
                    out=acc[:, : j1 - j0],
                    lhsT=w1_codes[b][:, a, i * P : (i + 1) * P].bitcast(FP8X4),
                    lhsT_scale=w1_sc[b][:, a, i * P : (i + 1) * P],
                    rhs=v_w[a][:, j0:j1].bitcast(FP8X4),
                    rhs_scale=v_sc[4 * a : P, j0:j1],
                    start=(a == 0),
                    stop=(a == 1),
                )
            nc.scalar.activation(out=h[:, j0:j1], in_=acc[:, : j1 - j0], func=TANH, bias=bias[:, b, i : i + 1])

        def weigh(s, h, j0, j1):
            b, i = divmod(s, PACK)
            nc.scalar.activation(out=h[:, j0:j1], in_=h[:, j0:j1], func=COPY, scale=gains[:, b, i : i + 1])

        def make_h(s, h):
            for j0 in range(0, S, BANK):
                tanh_part(s, h, j0, j0 + BANK)
            weigh(s, h, 0, S)

        def scatter(s, h, j0, j1):
            nc.vector.tensor_tensor(
                pages[s][:].indirect(entries(list2, j0, j1)), h[:, j0:j1], wgs_sb[s % PACK][:, j0:j1], MULT
            )

        def gather(s, dst, j0, j1):
            nc.vector.tensor_tensor(dst, pages[s][:].indirect(entries(list3, j0, j1)), wgt_sb[:, j0:j1], MULT)

        def interleave(planes, width):
            grouped = ring.tile([P, PACK * K_PASS], BF16, name="grouped", tag="grouped", align_bytes=64)
            nc.scalar.copy(
                out=grouped[:, : PACK * width].rearrange("p (j i) -> p j i", i=PACK),
                in_=planes.rearrange("p i j -> p j i"),
            )
            return grouped

        x_codes = [keep.tile([P, S], U32, name=f"x_codes{b}", align_bytes=64) for b in range(2)]
        x_sc = [keep.tile([P, S], U8, name=f"x_sc{b}", align_bytes=64) for b in range(2)]

        def quantize_x(b, grouped, j0, j1):
            nc.vector.quantize_mx(
                out=x_codes[b][:, j0:j1].bitcast(FP8X4), scales=x_sc[b][:, j0:j1], in_=grouped[:, : PACK * (j1 - j0)]
            )

        planes = keep.tile([P, PACK, S], F32, name="planes", align_bytes=64)

        def h_buffer(s):
            if s in (3, 4):
                return planes[:, s - 1, :]
            return keep.tile([P, S], F32, name=f"h{s}", tag=f"h{s % 5}")[:]

        h_of = [h_buffer(s) for s in range(2 * PACK)]

        for j0, j1 in FIRST_PARTS:
            tanh_part(0, h_of[0], j0, j1)
            weigh(0, h_of[0], j0, j1)
            scatter(0, h_of[0], j0, j1)
        for s in range(1, PACK):
            make_h(s, h_of[s])
        for a in range(2):
            round_w1(a, 1, planes[:, a, :].bitcast(BF16), nc.scalar.copy)
        nc.vector.quantize_mx(
            out=w1_codes[1][:].rearrange("p a c -> p (a c)").bitcast(FP8X4),
            scales=w1_sc[1][:].rearrange("p a c -> p (a c)"),
            in_=planes[:, 0:2, :].rearrange("p a j -> p (a j)").bitcast(BF16),
        )
        for s in range(PACK, 2 * PACK):
            pages.append(load_page(s))
            make_h(s, h_of[s])

        total = keep.tile([P, N // P, S], F32, name="total", tag="tab_w0")
        for nb in range(N // P):
            for j0 in range(0, S, BANK):
                cols = slice(j0, j0 + BANK)
                acc = next_bank()
                for a in range(2):
                    nc.tensor.matmul_mx(
                        out=acc[:],
                        lhsT=w3_w[:, a, nb * P : (nb + 1) * P].bitcast(FP8X4),
                        lhsT_scale=w_sc[:, 0, a, nb * P : (nb + 1) * P],
                        rhs=v_w[a][:, cols].bitcast(FP8X4),
                        rhs_scale=v_sc[4 * a : P, cols],
                        start=(a == 0),
                        stop=(a == 1),
                    )
                nc.scalar.copy(out=total[:, nb, cols], in_=acc[:])

        def y_pass(b, bank, nbs, j0, j1):
            for n, nb in enumerate(nbs):
                nc.tensor.matmul_mx(
                    out=bank[:, n * (j1 - j0) : (n + 1) * (j1 - j0)],
                    lhsT=w2_w[:, b, 2 * nb * P : 2 * (nb + 1) * P].bitcast(FP4X4),
                    lhsT_scale=w_sc[:, 1, b, nb * P : (nb + 1) * P],
                    rhs=x_codes[b][:, j0:j1].bitcast(FP8X4),
                    rhs_scale=x_sc[b][:, j0:j1],
                    start=(b == 0 and n == 0),
                    stop=(b == 1 and n == len(nbs) - 1),
                )

        for s in range(1, PACK + 1):
            scatter(s, h_of[s], 0, S)
            gather(s - 1, planes[:, s - 1, :], 0, S)
        for j0 in range(0, S, BANK):
            quantize_x(0, interleave(planes[:, :, j0 : j0 + BANK], BANK), j0, j0 + BANK)

        starts = [sum(CHUNKS[:c]) for c in range(len(CHUNKS))]
        y_banks = []
        for j0, width in zip(starts, CHUNKS):
            per_bank = BANK // width
            y_banks.append([(next_bank(), range(nb, nb + per_bank)) for nb in range(0, N // P, per_bank)])
            for bank, nbs in y_banks[-1]:
                y_pass(0, bank, nbs, j0, j0 + width)

        for s in range(PACK + 1, 2 * PACK):
            scatter(s, h_of[s], 0, S)

        out_blocks = out.rearrange("(nb p) j -> p nb j", p=P)
        spare = (h_of[-1], wgs_sb[-1][:])
        for c, (j0, width, chunk_banks) in enumerate(zip(starts, CHUNKS, y_banks)):
            j1 = j0 + width
            late = spare[c % 2][:, : PACK * width].rearrange("p (i j) -> p i j", i=PACK)
            for i in range(PACK):
                gather(PACK + i, late[:, i, :], j0, j1)
            quantize_x(1, interleave(late, width), j0, j1)
            for bank, nbs in chunk_banks:
                y_pass(1, bank, nbs, j0, j1)
                bounded = ring.tile([P, BANK], F32, name="bounded", bufs=3)
                nc.scalar.activation(out=bounded[:], in_=bank[:], func=TANH)
                part = total[:, nbs.start : nbs.stop, j0:j1]
                nc.vector.tensor_tensor(part, bounded[:].rearrange("p (n j) -> p n j", j=width), part, ADD)
                nc.sync.dma_start(out=out_blocks[:, nbs.start : nbs.stop, j0:j1], in_=part)
